import numpy as np
import ml_dtypes


def mxq(x, axis, fmt="e4m3"):
    dtype, down = {"e4m3": (ml_dtypes.float8_e4m3fn, 7), "e5m2": (ml_dtypes.float8_e5m2, 14)}[fmt]
    v = np.moveaxis(np.asarray(x, np.float32).astype(ml_dtypes.bfloat16).astype(np.float64), axis, -1)
    blocks = v.reshape(v.shape[:-1] + (-1, 32))
    amax = np.abs(blocks).max(-1, keepdims=True)
    byte = np.maximum(np.where(amax > 0, np.frexp(amax)[1] - 1 + 127, 0) - down, 1)
    scale = np.exp2(byte - 127.0)
    codes = (blocks / scale).astype(np.float32).astype(dtype).astype(np.float64)
    return np.moveaxis((codes * scale).reshape(v.shape), -1, axis)


WIDE = False


def mx_kscale(k):
    if not WIDE:
        return np.ones(k)
    levels = np.array([10, -10, 5, -5, 0])
    if k % 512:
        return np.exp2(np.random.permutation(np.resize(levels, k // 32))).repeat(32)
    a = np.empty((k // 512, 16))
    for p in range(k // 512):
        a[p, :8] = np.random.permutation(np.resize(levels, 8))
        for g in range(8):
            far = levels[np.abs(levels - a[p, g]) >= 10]
            a[p, g + 8] = far[np.random.randint(len(far))]
    return np.exp2(a.ravel()).repeat(32)


def f64(x):
    return np.asarray(x).astype(np.float64)


def striped(idx):
    return np.tile(idx.reshape(-1, 16).T, (8, 1)).astype(np.uint16)


def unstriped(offs):
    return offs[:16].T.reshape(-1).astype(np.int64)


def striped8(idx):
    return np.concatenate([x.reshape(-1, 16).T for x in idx]).astype(np.uint16)


def runs(offs, k):
    lists = np.stack([offs[16 * r : 16 * r + 16].T.reshape(-1) for r in range(8)]).astype(np.int64)
    return lists[np.arange(k) % 512 // 64]


def pack_weight(w):
    k, n = w.shape
    w = f64(np.asarray(w, np.float32).astype(ml_dtypes.bfloat16)).reshape(k // 32, 32, n)
    amax = np.abs(w).max(1)
    byte = np.clip(np.where(amax > 0, np.frexp(amax)[1] - 1 + 127 - 7, 1), 1, 254)
    scaled = (w * np.exp2(127.0 - byte)[:, None, :]).reshape(k, n).astype(np.float32)
    words = np.ascontiguousarray(scaled.reshape(k // 512, 128, 4, n).transpose(0, 1, 3, 2)).astype(ml_dtypes.float8_e4m3fn).view(np.uint8)
    return words, np.ascontiguousarray(byte.astype(np.uint8).reshape(k // 512, 16, n))


def unpack_weight(words, scales):
    g, p, n, _ = words.shape
    vals = np.ascontiguousarray(words).view(ml_dtypes.float8_e4m3fn).astype(np.float64) * np.repeat(np.exp2(scales.astype(np.float64) - 127.0), 8, axis=1)[..., None]
    return vals.transpose(0, 1, 3, 2).reshape(g * 512, n)

def planes(y):
    n, m = y.shape
    v = y.astype(np.float32).astype(ml_dtypes.bfloat16).astype(np.float64).reshape(n // 32, 32, m)
    top = np.abs(v).max(1)
    byte = np.clip(np.where(top > 0, np.frexp(top)[1] - 1 + 127 - 7, 1), 1, 254)
    codes = (v * np.exp2(127.0 - byte)[:, None, :]).reshape(n, m).astype(np.float32).astype(ml_dtypes.float8_e4m3fn).view(np.uint8)
    words = codes.reshape(n // 512, 128, 4, m).transpose(0, 1, 3, 2)
    return np.ascontiguousarray(words), np.ascontiguousarray(byte.astype(np.uint8).reshape(n // 512, 16, m))


K, T, S, V, U, H = 512, 2048, 512, 512, 1024, 512


def setup_inputs():
    n = np.random.standard_normal
    s = mx_kscale(K)[:, None]
    u = mx_kscale(S)
    packed_xT = pack_weight(n((K, T)) * s)
    packed_w1 = pack_weight(n((K, H)) / np.sqrt(K) / s)
    packed_w2 = pack_weight(n((K, H)) / np.sqrt(K) / s)
    return {
        "x_words": packed_xT[0],
        "x_scales": packed_xT[1],
        "w1_words": packed_w1[0],
        "w1_scales": packed_w1[1],
        "w2_words": packed_w2[0],
        "w2_scales": packed_w2[1],
        "ga": (np.random.uniform(0.5, 1.5, (H, 1)) * u[:, None]).astype(np.float32),
        "gb": (np.random.uniform(0.5, 1.5, (H, 1)) / u[:, None]).astype(np.float32),
        "page": n((S, U)).astype(np.float32),
        "offs": striped(np.random.permutation(T)[:S]),
        "two": striped(np.random.permutation(T)[:V]),
        "slot": striped8(np.stack([np.random.permutation(U)[:V] for _ in range(8)])),
    }


def reference(x_words, x_scales, w1_words, w1_scales, w2_words, w2_scales, ga, gb, page, offs, two, slot):
    xq = unpack_weight(x_words, x_scales)[:, unstriped(offs)]
    a = unpack_weight(w1_words, w1_scales).T @ xq
    z = f64(ga) * a
    x_two = unpack_weight(x_words, x_scales)[:, unstriped(two)]
    b = unpack_weight(w2_words, w2_scales).T @ x_two
    z2 = f64(gb) * b
    cv = 0.0625 * ((mxq(z, 0, "e4m3").T @ mxq(z2, 0, "e4m3")))
    tc = np.tanh(cv)
    out = f64(page).copy()
    out[np.arange(S)[:, None], runs(slot, S)] = tc
    return (out,) + planes(out)

@@ -1,0 +1,271 @@
+from contextlib import ExitStack
+
+import concourse.mybir as mybir
+from concourse.masks import make_identity
+
+K, T, S, V, U, H = 512, 2048, 512, 512, 1024, 512
+FLOPS = 2 * K * H * S + 2 * K * H * V + 2 * H * S * V
+
+F32 = mybir.dt.float32
+BF16 = mybir.dt.bfloat16
+I32 = mybir.dt.int32
+U32 = mybir.dt.uint32
+U16 = mybir.dt.uint16
+U8 = mybir.dt.uint8
+FP8X4 = mybir.dt.float8_e4m3fn_x4
+ACT = mybir.ActivationFunctionType
+MULT = mybir.AluOpType.mult
+
+P = 128
+PACK = 4
+QUADS = 4
+LIST_ROWS = 16
+HALF = 256
+QUARTER = 128
+
+
+def as_words(packed):
+    return packed[0].rearrange("p n r -> p (n r)").bitcast(I32)
+
+
+def load_scale_rows_repeated(queue, plane, scales):
+    for q in range(QUADS):
+        queue.dma_start(
+            out=plane[32 * q : 32 * (q + 1), :].bitcast(I32),
+            in_=scales[0, 4 * q : 4 * q + 4, :].bitcast(I32).unsqueeze(0).to_broadcast([8, 4, scales.shape[2] // 4]),
+        )
+
+
+def load_scale_rows(queue, plane, scales):
+    for q in range(QUADS):
+        queue.dma_start(
+            out=plane[32 * q : 32 * q + 4, :].bitcast(I32),
+            in_=scales[0, 4 * q : 4 * q + 4, :].bitcast(I32),
+        )
+
+
+def entries(offsets, start, count):
+    return offsets[:, start // LIST_ROWS : (start + count) // LIST_ROWS]
+
+
+def interleave(copy, grouped, rows):
+    copy(
+        out=grouped.rearrange("p (c i) t -> p c t i", i=4),
+        in_=rows.rearrange("p t (c i) -> p c t i", i=4),
+    )
+
+
+def tile_picked_momput_none_po_kernel(
+    tc, x_words, x_scales, w1_words, w1_scales, w2_words, w2_scales, ga, gb, page, offs, two, slot, out_0, out_1, out_2
+):
+    nc = tc.nc
+    with ExitStack() as ctx:
+        lists = ctx.enter_context(tc.tile_pool(name="lists", bufs=1))
+        keep = ctx.enter_context(tc.tile_pool(name="keep", bufs=1))
+        psum = ctx.enter_context(tc.psum_pool(name="psum", bufs=1))
+
+        def sb(name, shape, dtype, tag=None):
+            return keep.tile(shape, dtype, name=name, tag=tag or name, align_bytes=64)
+
+        offs_t = lists.tile([P, S // LIST_ROWS], U16, name="offs_t")
+        two_t = lists.tile([P, V // LIST_ROWS], U16, name="two_t")
+        slot_t = lists.tile([P, V // LIST_ROWS], U16, name="slot_t")
+
+        order = [0, 2, 3, 1]
+        identity = sb("identity", [P, P], F32)
+        xs = sb("xs", [P, T], U8, tag="slot0")
+        ws_raw = [sb(f"ws_raw{i}", [P, H], U8) for i in range(2)]
+        gain_rows = sb("gain_rows", [P, P], F32)
+        nc.vector.memset(gain_rows[:], 0.0)
+        nc.vector.memset(ws_raw[1][:].bitcast(I32), 0)
+        nc.vector.memset(ws_raw[0][:].bitcast(I32), 0)
+
+        xw = sb("xw", [P, T], U32, tag="slot3")
+        w_raw = [sb(f"w_raw{i}", [P, H], U32, tag=f"slot{2 - i}") for i in range(2)]
+        w_dealt = [sb(f"w_dealt{i}", [P, H], U32) for i in range(2)]
+        ws_dealt = [sb(f"ws_dealt{i}", [P, H], U8) for i in range(2)]
+        gains = sb("gains", [P, 2 * PACK], F32)
+        gain = [gains[:, i * PACK : (i + 1) * PACK] for i in range(2)]
+
+        nc.sync.dma_start(offs_t[:], offs)
+        load_scale_rows_repeated(nc.sync, xs, x_scales)
+        nc.sync.dma_start(two_t[:], two)
+        nc.sync.dma_start(out=xw[:].bitcast(I32), in_=as_words(x_words))
+        nc.sync.dma_start(out=w_raw[1][:].bitcast(I32), in_=as_words(w2_words))
+        nc.gpsimd.dma_start(out=w_raw[0][:].bitcast(I32), in_=as_words(w1_words))
+        for i, g_in in enumerate((ga, gb)):
+            nc.gpsimd.dma_start(
+                out=gain_rows[i * PACK : (i + 1) * PACK, :].rearrange("t (g j) -> t g j", j=8),
+                in_=g_in.rearrange("(g t j) o -> t g (j o)", t=PACK, j=8),
+            )
+        make_identity(nc, identity[:])
+        load_scale_rows(nc.sync, ws_raw[1], w2_scales)
+        load_scale_rows(nc.sync, ws_raw[0], w1_scales)
+        nc.sync.dma_start(slot_t[:], slot)
+        gain_bank = psum.tile([P, P], F32, name="gain_bank", tag="z1")
+        nc.tensor.transpose(gain_bank[:], gain_rows[:], identity[:])
+        nc.scalar.copy(out=gains[:], in_=gain_bank[:, 0 : 2 * PACK])
+        page_rows = page.rearrange("(p t) c -> p t c", t=PACK)
+        out_rows = out_0.rearrange("(p t) c -> p t c", t=PACK)
+
+        def deal(i):
+            nc.scalar.copy(
+                out=ws_dealt[i][:].bitcast(U32).rearrange("p (t g j) -> p t g j", t=PACK, j=2),
+                in_=ws_raw[i][:].bitcast(U32).rearrange("p (g t j) -> p t g j", t=PACK, j=2),
+            )
+            for t in range(0, PACK, 2):
+                nc.scalar.copy(
+                    out=w_dealt[i][:].rearrange("p (t g j) -> p t g j", t=PACK, j=8)[:, t : t + 2],
+                    in_=w_raw[i][:].rearrange("p (g t j) -> p t g j", t=PACK, j=8)[:, t : t + 2],
+                )
+
+        deal(1)
+        deal(0)
+
+        xa_w = sb("xa_w", [P, S], U32)
+        xa_s = sb("xa_s", [P, S], U8)
+        xb_w = sb("xb_w", [P, V], U32)
+        xb_s = sb("xb_s", [P, V], U8)
+        xd_w = sb("xd_w", [P, S], U32)
+        xd_s = sb("xd_s", [P, S], U8)
+
+        def deal_tokens(dealt, picked):
+            nc.vector.tensor_copy(
+                out=dealt[:].rearrange("p (r c i) -> p c r i", r=PACK, i=4),
+                in_=picked[:].rearrange("p (c i r) -> p c r i", r=PACK, i=4),
+            )
+
+        nc.vector.tensor_copy(xa_s[:], xs[:].indirect(offs_t[:]))
+        nc.vector.tensor_copy(xb_s[:], xs[:].indirect(two_t[:]))
+        deal_tokens(xd_s, xa_s)
+        nc.vector.tensor_copy(xb_w[:, 0:HALF], xw[:].indirect(entries(two_t, 0, HALF)))
+        nc.vector.tensor_copy(xa_w[:], xw[:].indirect(offs_t[:]))
+        nc.vector.tensor_copy(xb_w[:, HALF:], xw[:].indirect(entries(two_t, HALF, HALF)))
+        deal_tokens(xd_w, xa_w)
+
+        window = {}
+        for n, t in enumerate(order):
+            window[t] = sb(f"window{t}", [P, U], F32, tag=f"slot{n}")
+            nc.sync.dma_start(out=window[t][:], in_=page_rows[:, t, :])
+
+        def product(out, lw, ls, rw, rs):
+            nc.tensor.matmul_mx(
+                out=out, lhsT=lw.bitcast(FP8X4), lhsT_scale=ls, rhs=rw.bitcast(FP8X4), rhs_scale=rs, start=True, stop=True
+            )
+
+        def project(out, i, t, words, scales, start, count):
+            wcols = slice(t * P, (t + 1) * P)
+            cols = slice(start, start + count)
+            product(out, w_dealt[i][:, wcols], ws_dealt[i][:, wcols], words[:, cols], scales[:, cols])
+
+        bq_bank = [psum.tile([P, PACK, QUARTER], F32, name=f"bq_bank{q}", tag=f"bq{q}") for q in range(2)]
+        for q in range(2):
+            for t in range(PACK):
+                project(bq_bank[q][:, t, :], 1, t, xb_w, xb_s, q * QUARTER, QUARTER)
+        a_bank = {r: psum.tile([P, PACK, P], F32, name=f"a_bank{r}", tag=f"z{r}") for r in order}
+
+        def project_tokens(r):
+            for t in range(PACK):
+                project(a_bank[r][:, t, :], 0, t, xd_w, xd_s, r * P, P)
+
+        project_tokens(order[0])
+        bh_bank = [psum.tile([P, 2, HALF], F32, name=f"bh_bank{u}", tag=f"bh{u}") for u in range(2)]
+        for t in range(PACK):
+            project(bh_bank[t // 2][:, t % 2, :], 1, t, xb_w, xb_s, HALF, HALF)
+        for r in order[1:]:
+            project_tokens(r)
+
+        z_rows = {r: sb(f"z_rows{r}", [P, PACK, P], BF16) for r in order[1:]}
+        z_grp = {r: sb(f"z_grp{r}", [P, P, PACK], BF16) for r in order}
+        z_w = sb("z_w", [P, S], U32)
+        z_s = sb("z_s", [P, S], U8)
+        z2_grp = [sb(f"z2_grp{q}", [P, QUARTER, PACK], BF16) for q in range(2)]
+        z2_rows = sb("z2_rows", [P, PACK, HALF], BF16)
+        z2_grph = sb("z2_grph", [P, HALF, PACK], BF16)
+        z2_w = sb("z2_w", [P, V], U32)
+        z2_s = sb("z2_s", [P, V], U8)
+
+        def quantise(words, scales, grouped):
+            nc.vector.quantize_mx(out=words.bitcast(FP8X4), scales=scales, in_=grouped.rearrange("p c t -> p (c t)"))
+
+        def weigh_and_group(grouped, bank, i):
+            nc.vector.tensor_tensor(
+                out=grouped[:],
+                in0=bank[:].rearrange("p t n -> p n t"),
+                in1=gain[i].unsqueeze(1).to_broadcast([P, P, PACK]),
+                op=MULT,
+            )
+
+        def z_quantise(r):
+            quantise(z_w[:, r * P : (r + 1) * P], z_s[:, r * P : (r + 1) * P], z_grp[r][:])
+
+        for q in range(2):
+            weigh_and_group(z2_grp[q], bq_bank[q], 1)
+        weigh_and_group(z_grp[order[0]], a_bank[order[0]], 0)
+        for q in range(2):
+            cols = slice(q * QUARTER, (q + 1) * QUARTER)
+            quantise(z2_w[:, cols], z2_s[:, cols], z2_grp[q][:])
+        z_quantise(order[0])
+        for t in range(PACK):
+            nc.scalar.activation(
+                out=z2_rows[:, t, :], in_=bh_bank[t // 2][:, t % 2, :], func=ACT.Copy, scale=gain[1][:, t : t + 1]
+            )
+        interleave(nc.vector.tensor_copy, z2_grph[:], z2_rows[:])
+        quantise(z2_w[:, HALF:], z2_s[:, HALF:], z2_grph[:])
+
+        y_grp = [sb(f"y_grp{h}", [P, U // 2, PACK], BF16) for h in range(2)]
+        y_w = sb("y_w", [P, U], U32)
+        y_s = sb("y_s", [P, U], U8)
+
+        def score(t, start, count, bank_tag):
+            lw, ls = z_w[:, t * P : (t + 1) * P], z_s[:, t * P : (t + 1) * P]
+            cols = slice(start, start + count)
+            bank = psum.tile([P, count], F32, name=f"cv{t}_{start}", tag=bank_tag)
+            product(bank[:], lw, ls, z2_w[:, cols], z2_s[:, cols])
+            values = sb(f"tc{t}_{start}", [P, count], F32, tag="slot0" if t == order[-1] else None)
+            nc.scalar.activation(out=values[:], in_=bank[:], func=ACT.Tanh, scale=0.0625)
+            return values
+
+        def put(t, start, count, values):
+            nc.vector.tensor_copy(window[t][:].indirect(entries(slot_t, start, count)), values[:])
+
+        def regroup(copy, t, h):
+            copy(out=y_grp[h][:, :, t], in_=window[t][:, h * (U // 2) : (h + 1) * (U // 2)])
+
+        def z_prepare(r):
+            for t in range(PACK):
+                nc.scalar.activation(
+                    out=z_rows[r][:, t, :], in_=a_bank[r][:, t, :], func=ACT.Copy, scale=gain[0][:, t : t + 1]
+                )
+            interleave(nc.scalar.copy, z_grp[r][:], z_rows[r][:])
+            z_quantise(r)
+
+        first = score(0, 0, HALF, "bq0")
+        z_prepare(order[1])
+        second = score(0, HALF, HALF, "bq1")
+        z_prepare(order[2])
+        rest = {order[1]: score(order[1], 0, V, "bh0")}
+        z_prepare(order[3])
+        rest[order[2]] = score(order[2], 0, V, "bh1")
+        put(0, 0, HALF, first)
+        put(0, HALF, HALF, second)
+        nc.sync.dma_start(out=out_rows[:, 0, :], in_=window[0][:])
+        for n, t in enumerate(order[1:]):
+            for h in range(2):
+                regroup(nc.scalar.copy, order[n], h)
+            if n == 0:
+                rest[order[-1]] = score(order[-1], 0, V, "z0")
+            put(t, 0, V, rest[t])
+            nc.sync.dma_start(out=out_rows[:, t, :], in_=window[t][:])
+        words_out = as_words(out_1)
+        for h in range(2):
+            regroup(nc.vector.tensor_copy, order[-1], h)
+        for h in range(2):
+            cols = slice(h * (U // 2), (h + 1) * (U // 2))
+            quantise(y_w[:, cols], y_s[:, cols], y_grp[h][:])
+            nc.sync.dma_start(out=words_out[:, cols], in_=y_w[:, cols].bitcast(I32))
+        for q in range(QUADS):
+            queue = nc.scalar if q % 2 else nc.sync
+            queue.dma_start(
+                out=out_2[0, 4 * q : 4 * q + 4, :].bitcast(I32), in_=y_s[32 * q : 32 * q + 4, :].bitcast(I32)
+            )

@@ -36,9 +36,9 @@ def load_scale_rows_repeated(queue, plane, scales):
         )
 
 
-def load_scale_rows(queue, plane, scales):
+def load_scale_rows(queues, plane, scales):
     for q in range(QUADS):
-        queue.dma_start(
+        queues[q].dma_start(
             out=plane[32 * q : 32 * q + 4, :].bitcast(I32),
             in_=scales[0, 4 * q : 4 * q + 4, :].bitcast(I32),
         )
@@ -76,9 +76,9 @@ def tile_picked_momput_none_po_kernel(
         xs = sb("xs", [P, T], U8, tag="slot0")
         ws_raw = [sb(f"ws_raw{i}", [P, H], U8) for i in range(2)]
         gain_rows = sb("gain_rows", [P, P], F32)
-        nc.vector.memset(gain_rows[:], 0.0)
         nc.vector.memset(ws_raw[1][:].bitcast(I32), 0)
         nc.vector.memset(ws_raw[0][:].bitcast(I32), 0)
+        nc.vector.memset(gain_rows[:], 0.0)
 
         xw = sb("xw", [P, T], U32, tag="slot3")
         w_raw = [sb(f"w_raw{i}", [P, H], U32, tag=f"slot{2 - i}") for i in range(2)]
@@ -93,14 +93,14 @@ def tile_picked_momput_none_po_kernel(
         nc.sync.dma_start(out=xw[:].bitcast(I32), in_=as_words(x_words))
         nc.sync.dma_start(out=w_raw[1][:].bitcast(I32), in_=as_words(w2_words))
         nc.gpsimd.dma_start(out=w_raw[0][:].bitcast(I32), in_=as_words(w1_words))
+        load_scale_rows([nc.sync] * QUADS, ws_raw[1], w2_scales)
+        load_scale_rows([nc.sync, nc.sync, nc.gpsimd, nc.gpsimd], ws_raw[0], w1_scales)
+        make_identity(nc, identity[:])
         for i, g_in in enumerate((ga, gb)):
-            nc.gpsimd.dma_start(
+            nc.sync.dma_start(
                 out=gain_rows[i * PACK : (i + 1) * PACK, :].rearrange("t (g j) -> t g j", j=8),
                 in_=g_in.rearrange("(g t j) o -> t g (j o)", t=PACK, j=8),
             )
-        make_identity(nc, identity[:])
-        load_scale_rows(nc.sync, ws_raw[1], w2_scales)
-        load_scale_rows(nc.sync, ws_raw[0], w1_scales)
         nc.sync.dma_start(slot_t[:], slot)
         gain_bank = psum.tile([P, P], F32, name="gain_bank", tag="z1")
         nc.tensor.transpose(gain_bank[:], gain_rows[:], identity[:])
@@ -213,7 +213,8 @@ def tile_picked_momput_none_po_kernel(
         interleave(nc.vector.tensor_copy, z2_grph[:], z2_rows[:])
         quantise(z2_w[:, HALF:], z2_s[:, HALF:], z2_grph[:])
 
-        y_grp = [sb(f"y_grp{h}", [P, U // 2, PACK], BF16) for h in range(2)]
+        chunks = [slice(0, 512), slice(512, 768), slice(768, 1024)]
+        y_grp = sb("y_grp", [P, U, PACK], BF16)
         y_w = sb("y_w", [P, U], U32)
         y_s = sb("y_s", [P, U], U8)
 
@@ -229,8 +230,8 @@ def tile_picked_momput_none_po_kernel(
         def put(t, start, count, values):
             nc.vector.tensor_copy(window[t][:].indirect(entries(slot_t, start, count)), values[:])
 
-        def regroup(copy, t, h):
-            copy(out=y_grp[h][:, :, t], in_=window[t][:, h * (U // 2) : (h + 1) * (U // 2)])
+        def regroup(copy, t, cols):
+            copy(out=y_grp[:, cols, t], in_=window[t][:, cols])
 
         def z_prepare(r):
             for t in range(PACK):
@@ -252,17 +253,16 @@ def tile_picked_momput_none_po_kernel(
         nc.sync.dma_start(out=out_rows[:, 0, :], in_=window[0][:])
         for n, t in enumerate(order[1:]):
             for h in range(2):
-                regroup(nc.scalar.copy, order[n], h)
+                regroup(nc.scalar.copy, order[n], slice(h * (U // 2), (h + 1) * (U // 2)))
             if n == 0:
                 rest[order[-1]] = score(order[-1], 0, V, "z0")
             put(t, 0, V, rest[t])
             nc.sync.dma_start(out=out_rows[:, t, :], in_=window[t][:])
         words_out = as_words(out_1)
         for h in range(2):
-            regroup(nc.vector.tensor_copy, order[-1], h)
-        for h in range(2):
-            cols = slice(h * (U // 2), (h + 1) * (U // 2))
-            quantise(y_w[:, cols], y_s[:, cols], y_grp[h][:])
+            regroup(nc.vector.tensor_copy, order[-1], slice(h * (U // 2), (h + 1) * (U // 2)))
+        for cols in chunks:
+            quantise(y_w[:, cols], y_s[:, cols], y_grp[:, cols, :])
             nc.sync.dma_start(out=words_out[:, cols], in_=y_w[:, cols].bitcast(I32))
         for q in range(QUADS):
             queue = nc.scalar if q % 2 else nc.sync

@@ -14,258 +14,263 @@ U16 = mybir.dt.uint16
 U8 = mybir.dt.uint8
 FP8X4 = mybir.dt.float8_e4m3fn_x4
 ACT = mybir.ActivationFunctionType
-MULT = mybir.AluOpType.mult
 
 P = 128
 PACK = 4
-QUADS = 4
+QUADRANT = 32
+BLOCK_ROWS = 8
 LIST_ROWS = 16
-HALF = 256
-QUARTER = 128
+HALF = V // 2
+LINE = 4
+
+ROW_TILES = [0, 2, 3, 1]
+VECTOR_COLUMNS = 768
+PIECES = [slice(0, 512), slice(512, 768), slice(768, 1024)]
 
 
 def as_words(packed):
     return packed[0].rearrange("p n r -> p (n r)").bitcast(I32)
 
 
-def load_scale_rows_repeated(queue, plane, scales):
-    for q in range(QUADS):
-        queue.dma_start(
-            out=plane[32 * q : 32 * (q + 1), :].bitcast(I32),
-            in_=scales[0, 4 * q : 4 * q + 4, :].bitcast(I32).unsqueeze(0).to_broadcast([8, 4, scales.shape[2] // 4]),
-        )
+def scale_rows(scales, quadrant):
+    return scales[0, PACK * quadrant : PACK * (quadrant + 1), :].bitcast(I32)
 
 
-def load_scale_rows(queues, plane, scales):
-    for q in range(QUADS):
-        queues[q].dma_start(
-            out=plane[32 * q : 32 * q + 4, :].bitcast(I32),
-            in_=scales[0, 4 * q : 4 * q + 4, :].bitcast(I32),
-        )
+def live_rows(plane, quadrant):
+    return plane[QUADRANT * quadrant : QUADRANT * quadrant + PACK, :].bitcast(I32)
 
 
 def entries(offsets, start, count):
     return offsets[:, start // LIST_ROWS : (start + count) // LIST_ROWS]
 
 
-def interleave(copy, grouped, rows):
-    copy(
-        out=grouped.rearrange("p (c i) t -> p c t i", i=4),
-        in_=rows.rearrange("p t (c i) -> p c t i", i=4),
-    )
+def block(index, width):
+    return slice(index * width, (index + 1) * width)
 
 
 def tile_picked_momput_none_po_kernel(
     tc, x_words, x_scales, w1_words, w1_scales, w2_words, w2_scales, ga, gb, page, offs, two, slot, out_0, out_1, out_2
 ):
     nc = tc.nc
+    first, second, third, last = ROW_TILES
+    quadrants = range(P // QUADRANT)
     with ExitStack() as ctx:
         lists = ctx.enter_context(tc.tile_pool(name="lists", bufs=1))
         keep = ctx.enter_context(tc.tile_pool(name="keep", bufs=1))
         psum = ctx.enter_context(tc.psum_pool(name="psum", bufs=1))
 
-        def sb(name, shape, dtype, tag=None):
-            return keep.tile(shape, dtype, name=name, tag=tag or name, align_bytes=64)
+        def sbuf(name, shape, dtype, after=None):
+            return keep.tile(shape, dtype, name=name, tag=after or name, align_bytes=64)
 
         offs_t = lists.tile([P, S // LIST_ROWS], U16, name="offs_t")
         two_t = lists.tile([P, V // LIST_ROWS], U16, name="two_t")
         slot_t = lists.tile([P, V // LIST_ROWS], U16, name="slot_t")
 
-        order = [0, 2, 3, 1]
-        identity = sb("identity", [P, P], F32)
-        xs = sb("xs", [P, T], U8, tag="slot0")
-        ws_raw = [sb(f"ws_raw{i}", [P, H], U8) for i in range(2)]
-        gain_rows = sb("gain_rows", [P, P], F32)
-        nc.vector.memset(ws_raw[1][:].bitcast(I32), 0)
-        nc.vector.memset(ws_raw[0][:].bitcast(I32), 0)
+        identity = sbuf("identity", [P, P], F32)
+        x_plane = sbuf("x_plane", [P, T], U8)
+        x_codes = sbuf("x_codes", [P, T], U32)
+        w_plane = [sbuf(f"w_plane{i}", [P, H], U8) for i in range(2)]
+        w_codes = [sbuf(f"w_codes{i}", [P, H], U32) for i in range(2)]
+        w_plane_dealt = [sbuf(f"w_plane_dealt{i}", [P, H], U8) for i in range(2)]
+        w_codes_dealt = [sbuf(f"w_codes_dealt{i}", [P, H], U32) for i in range(2)]
+        gain_rows = sbuf("gain_rows", [P, P], F32)
+        gains = sbuf("gains", [P, 2, PACK], F32)
+
         nc.vector.memset(gain_rows[:], 0.0)
+        for i in (1, 0):
+            nc.vector.memset(w_plane[i][:].bitcast(I32), 0)
 
-        xw = sb("xw", [P, T], U32, tag="slot3")
-        w_raw = [sb(f"w_raw{i}", [P, H], U32, tag=f"slot{2 - i}") for i in range(2)]
-        w_dealt = [sb(f"w_dealt{i}", [P, H], U32) for i in range(2)]
-        ws_dealt = [sb(f"ws_dealt{i}", [P, H], U8) for i in range(2)]
-        gains = sb("gains", [P, 2 * PACK], F32)
-        gain = [gains[:, i * PACK : (i + 1) * PACK] for i in range(2)]
-
-        nc.sync.dma_start(offs_t[:], offs)
-        load_scale_rows_repeated(nc.sync, xs, x_scales)
         nc.sync.dma_start(two_t[:], two)
-        nc.sync.dma_start(out=xw[:].bitcast(I32), in_=as_words(x_words))
-        nc.sync.dma_start(out=w_raw[1][:].bitcast(I32), in_=as_words(w2_words))
-        nc.gpsimd.dma_start(out=w_raw[0][:].bitcast(I32), in_=as_words(w1_words))
-        load_scale_rows([nc.sync] * QUADS, ws_raw[1], w2_scales)
-        load_scale_rows([nc.sync, nc.sync, nc.gpsimd, nc.gpsimd], ws_raw[0], w1_scales)
-        make_identity(nc, identity[:])
-        for i, g_in in enumerate((ga, gb)):
+        for q in quadrants:
             nc.sync.dma_start(
-                out=gain_rows[i * PACK : (i + 1) * PACK, :].rearrange("t (g j) -> t g j", j=8),
-                in_=g_in.rearrange("(g t j) o -> t g (j o)", t=PACK, j=8),
+                out=x_plane[block(q, QUADRANT), :].bitcast(I32),
+                in_=scale_rows(x_scales, q).unsqueeze(0).to_broadcast([QUADRANT // PACK, PACK, T // PACK]),
             )
+        nc.sync.dma_start(offs_t[:], offs)
+        nc.sync.dma_start(out=x_codes[:].bitcast(I32), in_=as_words(x_words))
+        make_identity(nc, identity[:])
+        nc.sync.dma_start(out=w_codes[1][:].bitcast(I32), in_=as_words(w2_words))
+        nc.sync.dma_start(out=w_codes[0][:].bitcast(I32), in_=as_words(w1_words))
+        for i, gain in enumerate((ga, gb)):
+            nc.sync.dma_start(
+                out=gain_rows[block(i, PACK), :].rearrange("t (g j) -> t g j", j=BLOCK_ROWS),
+                in_=gain.rearrange("(g t j) o -> t g (j o)", t=PACK, j=BLOCK_ROWS),
+            )
+        for i, scales in ((1, w2_scales), (0, w1_scales)):
+            for q in quadrants:
+                nc.sync.dma_start(out=live_rows(w_plane[i], q), in_=scale_rows(scales, q))
         nc.sync.dma_start(slot_t[:], slot)
-        gain_bank = psum.tile([P, P], F32, name="gain_bank", tag="z1")
-        nc.tensor.transpose(gain_bank[:], gain_rows[:], identity[:])
-        nc.scalar.copy(out=gains[:], in_=gain_bank[:, 0 : 2 * PACK])
-        page_rows = page.rearrange("(p t) c -> p t c", t=PACK)
-        out_rows = out_0.rearrange("(p t) c -> p t c", t=PACK)
 
-        def deal(i):
+        gain_bank = psum.tile([P, P], F32, name="gain_bank", tag=f"a{last}")
+        nc.tensor.transpose(gain_bank[:], gain_rows[:], identity[:])
+        nc.scalar.copy(out=gains[:].rearrange("p i t -> p (i t)"), in_=gain_bank[:, 0 : 2 * PACK])
+
+        for i in (1, 0):
             nc.scalar.copy(
-                out=ws_dealt[i][:].bitcast(U32).rearrange("p (t g j) -> p t g j", t=PACK, j=2),
-                in_=ws_raw[i][:].bitcast(U32).rearrange("p (g t j) -> p t g j", t=PACK, j=2),
+                out=w_plane_dealt[i][:].bitcast(U32).rearrange("p (t g j) -> p t g j", t=PACK, j=BLOCK_ROWS // 4),
+                in_=w_plane[i][:].bitcast(U32).rearrange("p (g t j) -> p t g j", t=PACK, j=BLOCK_ROWS // 4),
             )
-            for t in range(0, PACK, 2):
+            for slots in (slice(0, 2), slice(2, 4)):
                 nc.scalar.copy(
-                    out=w_dealt[i][:].rearrange("p (t g j) -> p t g j", t=PACK, j=8)[:, t : t + 2],
-                    in_=w_raw[i][:].rearrange("p (g t j) -> p t g j", t=PACK, j=8)[:, t : t + 2],
+                    out=w_codes_dealt[i][:].rearrange("p (t g j) -> p t g j", t=PACK, j=BLOCK_ROWS)[:, slots],
+                    in_=w_codes[i][:].rearrange("p (g t j) -> p t g j", t=PACK, j=BLOCK_ROWS)[:, slots],
                 )
 
-        deal(1)
-        deal(0)
-
-        xa_w = sb("xa_w", [P, S], U32)
-        xa_s = sb("xa_s", [P, S], U8)
-        xb_w = sb("xb_w", [P, V], U32)
-        xb_s = sb("xb_s", [P, V], U8)
-        xd_w = sb("xd_w", [P, S], U32)
-        xd_s = sb("xd_s", [P, S], U8)
+        a_codes = sbuf("a_codes", [P, S], U32)
+        a_plane = sbuf("a_plane", [P, S], U8)
+        a_codes_dealt = sbuf("a_codes_dealt", [P, S], U32)
+        a_plane_dealt = sbuf("a_plane_dealt", [P, S], U8)
+        b_codes = [sbuf(f"b_codes{half}", [P, HALF], U32) for half in range(2)]
+        b_plane = sbuf("b_plane", [P, V], U8)
 
         def deal_tokens(dealt, picked):
             nc.vector.tensor_copy(
-                out=dealt[:].rearrange("p (r c i) -> p c r i", r=PACK, i=4),
-                in_=picked[:].rearrange("p (c i r) -> p c r i", r=PACK, i=4),
+                out=dealt[:].rearrange("p (r c i) -> p c r i", r=PACK, i=LINE),
+                in_=picked[:].rearrange("p (c i r) -> p c r i", r=PACK, i=LINE),
             )
 
-        nc.vector.tensor_copy(xa_s[:], xs[:].indirect(offs_t[:]))
-        nc.vector.tensor_copy(xb_s[:], xs[:].indirect(two_t[:]))
-        deal_tokens(xd_s, xa_s)
-        nc.vector.tensor_copy(xb_w[:, 0:HALF], xw[:].indirect(entries(two_t, 0, HALF)))
-        nc.vector.tensor_copy(xa_w[:], xw[:].indirect(offs_t[:]))
-        nc.vector.tensor_copy(xb_w[:, HALF:], xw[:].indirect(entries(two_t, HALF, HALF)))
-        deal_tokens(xd_w, xa_w)
+        nc.vector.tensor_copy(b_plane[:], x_plane[:].indirect(two_t[:]))
+        nc.vector.tensor_copy(a_plane[:], x_plane[:].indirect(offs_t[:]))
+        deal_tokens(a_plane_dealt, a_plane)
+        nc.vector.tensor_copy(b_codes[0][:], x_codes[:].indirect(entries(two_t, 0, HALF)))
+        nc.vector.tensor_copy(a_codes[:], x_codes[:].indirect(offs_t[:]))
+        deal_tokens(a_codes_dealt, a_codes)
+        nc.vector.tensor_copy(b_codes[1][:], x_codes[:].indirect(entries(two_t, HALF, HALF)))
 
+        page_rows = page.rearrange("(p r) c -> p r c", r=PACK)
+        out_rows = out_0.rearrange("(p r) c -> p r c", r=PACK)
         window = {}
-        for n, t in enumerate(order):
-            window[t] = sb(f"window{t}", [P, U], F32, tag=f"slot{n}")
-            nc.sync.dma_start(out=window[t][:], in_=page_rows[:, t, :])
+        for r, freed in zip(ROW_TILES, ["w_codes1", "w_codes0", "a_codes", "x_codes"]):
+            window[r] = sbuf(f"window{r}", [P, U], F32, after=freed)
+            nc.sync.dma_start(out=window[r][:], in_=page_rows[:, r, :])
 
-        def product(out, lw, ls, rw, rs):
+        def product(out, left_codes, left_plane, right_codes, right_plane):
             nc.tensor.matmul_mx(
-                out=out, lhsT=lw.bitcast(FP8X4), lhsT_scale=ls, rhs=rw.bitcast(FP8X4), rhs_scale=rs, start=True, stop=True
+                out=out,
+                lhsT=left_codes.bitcast(FP8X4),
+                lhsT_scale=left_plane,
+                rhs=right_codes.bitcast(FP8X4),
+                rhs_scale=right_plane,
+                start=True,
+                stop=True,
             )
 
-        def project(out, i, t, words, scales, start, count):
-            wcols = slice(t * P, (t + 1) * P)
-            cols = slice(start, start + count)
-            product(out, w_dealt[i][:, wcols], ws_dealt[i][:, wcols], words[:, cols], scales[:, cols])
+        def project(out, i, t, codes, plane):
+            product(out, w_codes_dealt[i][:, block(t, P)], w_plane_dealt[i][:, block(t, P)], codes, plane)
 
-        bq_bank = [psum.tile([P, PACK, QUARTER], F32, name=f"bq_bank{q}", tag=f"bq{q}") for q in range(2)]
-        for q in range(2):
+        b_bank = [psum.tile([P, PACK, P], F32, name=f"b_bank{n}", tag=f"b{n}") for n in range(V // P)]
+        a_bank = {r: psum.tile([P, PACK, P], F32, name=f"a_bank{r}", tag=f"a{r}") for r in ROW_TILES}
+
+        def project_b(half):
+            for n in range(2):
+                for t in range(PACK):
+                    quarter = 2 * half + n
+                    project(b_bank[quarter][:, t, :], 1, t, b_codes[half][:, block(n, P)], b_plane[:, block(quarter, P)])
+
+        def project_a(r):
             for t in range(PACK):
-                project(bq_bank[q][:, t, :], 1, t, xb_w, xb_s, q * QUARTER, QUARTER)
-        a_bank = {r: psum.tile([P, PACK, P], F32, name=f"a_bank{r}", tag=f"z{r}") for r in order}
+                project(a_bank[r][:, t, :], 0, t, a_codes_dealt[:, block(r, P)], a_plane_dealt[:, block(r, P)])
 
-        def project_tokens(r):
-            for t in range(PACK):
-                project(a_bank[r][:, t, :], 0, t, xd_w, xd_s, r * P, P)
+        project_b(0)
+        project_a(first)
+        project_b(1)
+        for r in ROW_TILES[1:]:
+            project_a(r)
 
-        project_tokens(order[0])
-        bh_bank = [psum.tile([P, 2, HALF], F32, name=f"bh_bank{u}", tag=f"bh{u}") for u in range(2)]
-        for t in range(PACK):
-            project(bh_bank[t // 2][:, t % 2, :], 1, t, xb_w, xb_s, HALF, HALF)
-        for r in order[1:]:
-            project_tokens(r)
+        z_slots = {r: sbuf(f"z_slots{r}", [P, PACK, P], BF16) for r in ROW_TILES[1:]}
+        z_grouped = {r: sbuf(f"z_grouped{r}", [P, P, PACK], BF16) for r in ROW_TILES}
+        z_codes = sbuf("z_codes", [P, S], U32)
+        z_plane = sbuf("z_plane", [P, S], U8)
+        z2_grouped = [sbuf(f"z2_grouped{half}", [P, HALF, PACK], BF16) for half in range(2)]
+        z2_codes = sbuf("z2_codes", [P, V], U32)
+        z2_plane = sbuf("z2_plane", [P, V], U8)
 
-        z_rows = {r: sb(f"z_rows{r}", [P, PACK, P], BF16) for r in order[1:]}
-        z_grp = {r: sb(f"z_grp{r}", [P, P, PACK], BF16) for r in order}
-        z_w = sb("z_w", [P, S], U32)
-        z_s = sb("z_s", [P, S], U8)
-        z2_grp = [sb(f"z2_grp{q}", [P, QUARTER, PACK], BF16) for q in range(2)]
-        z2_rows = sb("z2_rows", [P, PACK, HALF], BF16)
-        z2_grph = sb("z2_grph", [P, HALF, PACK], BF16)
-        z2_w = sb("z2_w", [P, V], U32)
-        z2_s = sb("z2_s", [P, V], U8)
+        def quantise(codes, plane, grouped):
+            nc.vector.quantize_mx(out=codes.bitcast(FP8X4), scales=plane, in_=grouped.rearrange("p c t -> p (c t)"))
 
-        def quantise(words, scales, grouped):
-            nc.vector.quantize_mx(out=words.bitcast(FP8X4), scales=scales, in_=grouped.rearrange("p c t -> p (c t)"))
+        def quantise_z(r):
+            quantise(z_codes[:, block(r, P)], z_plane[:, block(r, P)], z_grouped[r][:])
+
+        def quantise_z2(half):
+            quantise(z2_codes[:, block(half, HALF)], z2_plane[:, block(half, HALF)], z2_grouped[half][:])
+
+        def weigh(slots, t, sums, i):
+            nc.scalar.activation(out=slots[:, t, :], in_=sums, func=ACT.Copy, scale=gains[:, i, t : t + 1])
+
+        def group(copy, grouped, slots):
+            copy(
+                out=grouped[:].rearrange("p (c i) t -> p c t i", i=LINE),
+                in_=slots[:].rearrange("p t (c i) -> p c t i", i=LINE),
+            )
 
         def weigh_and_group(grouped, bank, i):
             nc.vector.tensor_tensor(
-                out=grouped[:],
-                in0=bank[:].rearrange("p t n -> p n t"),
-                in1=gain[i].unsqueeze(1).to_broadcast([P, P, PACK]),
-                op=MULT,
+                out=grouped,
+                in0=bank[:].rearrange("p t c -> p c t"),
+                in1=gains[:, i, :].unsqueeze(1).to_broadcast([P, P, PACK]),
+                op=mybir.AluOpType.mult,
             )
 
-        def z_quantise(r):
-            quantise(z_w[:, r * P : (r + 1) * P], z_s[:, r * P : (r + 1) * P], z_grp[r][:])
+        def weigh_b(half):
+            for n in range(2):
+                weigh_and_group(z2_grouped[half][:, block(n, P), :], b_bank[2 * half + n], 1)
 
-        for q in range(2):
-            weigh_and_group(z2_grp[q], bq_bank[q], 1)
-        weigh_and_group(z_grp[order[0]], a_bank[order[0]], 0)
-        for q in range(2):
-            cols = slice(q * QUARTER, (q + 1) * QUARTER)
-            quantise(z2_w[:, cols], z2_s[:, cols], z2_grp[q][:])
-        z_quantise(order[0])
-        for t in range(PACK):
-            nc.scalar.activation(
-                out=z2_rows[:, t, :], in_=bh_bank[t // 2][:, t % 2, :], func=ACT.Copy, scale=gain[1][:, t : t + 1]
-            )
-        interleave(nc.vector.tensor_copy, z2_grph[:], z2_rows[:])
-        quantise(z2_w[:, HALF:], z2_s[:, HALF:], z2_grph[:])
+        def prepare_z(r):
+            for t in range(PACK):
+                weigh(z_slots[r], t, a_bank[r][:, t, :], 0)
+            group(nc.scalar.copy, z_grouped[r], z_slots[r])
+            quantise_z(r)
 
-        chunks = [slice(0, 512), slice(512, 768), slice(768, 1024)]
-        y_grp = sb("y_grp", [P, U, PACK], BF16)
-        y_w = sb("y_w", [P, U], U32)
-        y_s = sb("y_s", [P, U], U8)
+        weigh_b(0)
+        weigh_and_group(z_grouped[first][:], a_bank[first], 0)
+        quantise_z2(0)
+        quantise_z(first)
+        weigh_b(1)
+        quantise_z2(1)
 
-        def score(t, start, count, bank_tag):
-            lw, ls = z_w[:, t * P : (t + 1) * P], z_s[:, t * P : (t + 1) * P]
+        y_codes = sbuf("y_codes", [P, U], U32)
+        y_plane = sbuf("y_plane", [P, U], U8)
+
+        def score(r, start, count, bank, after=None):
             cols = slice(start, start + count)
-            bank = psum.tile([P, count], F32, name=f"cv{t}_{start}", tag=bank_tag)
-            product(bank[:], lw, ls, z2_w[:, cols], z2_s[:, cols])
-            values = sb(f"tc{t}_{start}", [P, count], F32, tag="slot0" if t == order[-1] else None)
-            nc.scalar.activation(out=values[:], in_=bank[:], func=ACT.Tanh, scale=0.0625)
+            cv = psum.tile([P, count], F32, name=f"cv{r}_{start}", tag=bank)
+            product(cv[:], z_codes[:, block(r, P)], z_plane[:, block(r, P)], z2_codes[:, cols], z2_plane[:, cols])
+            values = sbuf(f"tanh{r}_{start}", [P, count], F32, after=after)
+            nc.scalar.activation(out=values[:], in_=cv[:], func=ACT.Tanh, scale=0.0625)
             return values
 
-        def put(t, start, count, values):
-            nc.vector.tensor_copy(window[t][:].indirect(entries(slot_t, start, count)), values[:])
+        def put(r, start, count, values):
+            nc.vector.tensor_copy(window[r][:].indirect(entries(slot_t, start, count)), values[:])
 
-        def regroup(copy, t, cols):
-            copy(out=y_grp[:, cols, t], in_=window[t][:, cols])
+        first_half = score(first, 0, HALF, "b0")
+        prepare_z(second)
+        prepare_z(third)
+        second_half = score(first, HALF, HALF, "b1", after=f"z_slots{third}")
+        prepare_z(last)
+        values = {second: score(second, 0, V, "b2", after=f"z_slots{last}")}
+        values[third] = score(third, 0, V, "b2")
 
-        def z_prepare(r):
-            for t in range(PACK):
-                nc.scalar.activation(
-                    out=z_rows[r][:, t, :], in_=a_bank[r][:, t, :], func=ACT.Copy, scale=gain[0][:, t : t + 1]
-                )
-            interleave(nc.scalar.copy, z_grp[r][:], z_rows[r][:])
-            z_quantise(r)
+        y_grouped = sbuf("y_grouped", [P, U, PACK], BF16, after=f"z_grouped{last}")
 
-        first = score(0, 0, HALF, "bq0")
-        z_prepare(order[1])
-        second = score(0, HALF, HALF, "bq1")
-        z_prepare(order[2])
-        rest = {order[1]: score(order[1], 0, V, "bh0")}
-        z_prepare(order[3])
-        rest[order[2]] = score(order[2], 0, V, "bh1")
-        put(0, 0, HALF, first)
-        put(0, HALF, HALF, second)
-        nc.sync.dma_start(out=out_rows[:, 0, :], in_=window[0][:])
-        for n, t in enumerate(order[1:]):
-            for h in range(2):
-                regroup(nc.scalar.copy, order[n], slice(h * (U // 2), (h + 1) * (U // 2)))
-            if n == 0:
-                rest[order[-1]] = score(order[-1], 0, V, "z0")
-            put(t, 0, V, rest[t])
-            nc.sync.dma_start(out=out_rows[:, t, :], in_=window[t][:])
-        words_out = as_words(out_1)
-        for h in range(2):
-            regroup(nc.vector.tensor_copy, order[-1], slice(h * (U // 2), (h + 1) * (U // 2)))
-        for cols in chunks:
-            quantise(y_w[:, cols], y_s[:, cols], y_grp[:, cols, :])
-            nc.sync.dma_start(out=words_out[:, cols], in_=y_w[:, cols].bitcast(I32))
-        for q in range(QUADS):
+        def regroup(copy, r, cols):
+            copy(out=y_grouped[:, cols, r], in_=window[r][:, cols])
+
+        put(first, 0, HALF, first_half)
+        put(first, HALF, HALF, second_half)
+        nc.sync.dma_start(out=out_rows[:, first, :], in_=window[first][:])
+        for done, r in zip(ROW_TILES, ROW_TILES[1:]):
+            for half in range(2):
+                regroup(nc.scalar.copy, done, block(half, U // 2))
+            if done == first:
+                values[last] = score(last, 0, V, f"a{first}", after="w_codes1")
+            put(r, 0, V, values[r])
+            nc.sync.dma_start(out=out_rows[:, r, :], in_=window[r][:])
+
+        for cols in PIECES:
+            regroup(nc.vector.tensor_copy if cols.stop <= VECTOR_COLUMNS else nc.scalar.copy, last, cols)
+        for cols in PIECES:
+            quantise(y_codes[:, cols], y_plane[:, cols], y_grouped[:, cols, :])
+            nc.sync.dma_start(out=as_words(out_1)[:, cols], in_=y_codes[:, cols].bitcast(I32))
+        for q in quadrants:
             queue = nc.scalar if q % 2 else nc.sync
-            queue.dma_start(
-                out=out_2[0, 4 * q : 4 * q + 4, :].bitcast(I32), in_=y_s[32 * q : 32 * q + 4, :].bitcast(I32)
-            )
+            queue.dma_start(out=scale_rows(out_2, q), in_=live_rows(y_plane, q))

@@ -20,6 +20,7 @@ PACK = 4
 QUADRANT = 32
 BLOCK_ROWS = 8
 LIST_ROWS = 16
+SCORE_SCALE = 0.0625
 HALF = V // 2
 LINE = 4
 
@@ -79,6 +80,8 @@ def tile_picked_momput_none_po_kernel(
         nc.vector.memset(gain_rows[:], 0.0)
         for i in (1, 0):
             nc.vector.memset(w_plane[i][:].bitcast(I32), 0)
+        sixteenth = sbuf("sixteenth", [P, 1], F32)
+        nc.vector.memset(sixteenth[:], SCORE_SCALE)
 
         nc.sync.dma_start(two_t[:], two)
         for q in quadrants:
@@ -231,26 +234,26 @@ def tile_picked_momput_none_po_kernel(
         y_codes = sbuf("y_codes", [P, U], U32)
         y_plane = sbuf("y_plane", [P, U], U8)
 
-        def score(r, start, count, bank, after=None):
+        def score(r, start, count, bank, scale, after=None):
             cols = slice(start, start + count)
             cv = psum.tile([P, count], F32, name=f"cv{r}_{start}", tag=bank)
             product(cv[:], z_codes[:, block(r, P)], z_plane[:, block(r, P)], z2_codes[:, cols], z2_plane[:, cols])
             values = sbuf(f"tanh{r}_{start}", [P, count], F32, after=after)
-            nc.scalar.activation(out=values[:], in_=cv[:], func=ACT.Tanh, scale=0.0625)
+            nc.scalar.activation(out=values[:], in_=cv[:], func=ACT.Tanh, scale=scale)
             return values
 
         def put(r, start, count, values):
             nc.vector.tensor_copy(window[r][:].indirect(entries(slot_t, start, count)), values[:])
 
-        first_half = score(first, 0, HALF, "b0")
+        first_half = score(first, 0, HALF, "b0", sixteenth[:])
         prepare_z(second)
         prepare_z(third)
-        second_half = score(first, HALF, HALF, "b1", after=f"z_slots{third}")
+        second_half = score(first, HALF, HALF, "b1", sixteenth[:], after=f"z_slots{third}")
         prepare_z(last)
-        values = {second: score(second, 0, V, "b2", after=f"z_slots{last}")}
-        values[third] = score(third, 0, V, "b2")
+        values = {second: score(second, 0, V, "b2", sixteenth[:], after=f"z_slots{last}")}
+        values[third] = score(third, 0, V, "b3", sixteenth[:], after=f"z_grouped{last}")
 
-        y_grouped = sbuf("y_grouped", [P, U, PACK], BF16, after=f"z_grouped{last}")
+        y_grouped = sbuf("y_grouped", [P, U, PACK], BF16, after="sixteenth")
 
         def regroup(copy, r, cols):
             copy(out=y_grouped[:, cols, r], in_=window[r][:, cols])
@@ -259,10 +262,10 @@ def tile_picked_momput_none_po_kernel(
         put(first, HALF, HALF, second_half)
         nc.sync.dma_start(out=out_rows[:, first, :], in_=window[first][:])
         for done, r in zip(ROW_TILES, ROW_TILES[1:]):
-            for half in range(2):
-                regroup(nc.scalar.copy, done, block(half, U // 2))
+            for cols in ([slice(0, U)] if done == first else [block(half, U // 2) for half in range(2)]):
+                regroup(nc.scalar.copy, done, cols)
             if done == first:
-                values[last] = score(last, 0, V, f"a{first}", after="w_codes1")
+                values[last] = score(last, 0, V, "b3", SCORE_SCALE)
             put(r, 0, V, values[r])
             nc.sync.dma_start(out=out_rows[:, r, :], in_=window[r][:])
 

@@ -83,25 +83,26 @@ def tile_picked_momput_none_po_kernel(
         sixteenth = sbuf("sixteenth", [P, 1], F32)
         nc.vector.memset(sixteenth[:], SCORE_SCALE)
 
-        nc.sync.dma_start(two_t[:], two)
+        nc.sync.dma_start(offs_t[:], offs)
         for q in quadrants:
             nc.sync.dma_start(
                 out=x_plane[block(q, QUADRANT), :].bitcast(I32),
                 in_=scale_rows(x_scales, q).unsqueeze(0).to_broadcast([QUADRANT // PACK, PACK, T // PACK]),
             )
-        nc.sync.dma_start(offs_t[:], offs)
+        nc.sync.dma_start(two_t[:], two)
         nc.sync.dma_start(out=x_codes[:].bitcast(I32), in_=as_words(x_words))
         make_identity(nc, identity[:])
         nc.sync.dma_start(out=w_codes[1][:].bitcast(I32), in_=as_words(w2_words))
-        nc.sync.dma_start(out=w_codes[0][:].bitcast(I32), in_=as_words(w1_words))
         for i, gain in enumerate((ga, gb)):
             nc.sync.dma_start(
                 out=gain_rows[block(i, PACK), :].rearrange("t (g j) -> t g j", j=BLOCK_ROWS),
                 in_=gain.rearrange("(g t j) o -> t g (j o)", t=PACK, j=BLOCK_ROWS),
             )
-        for i, scales in ((1, w2_scales), (0, w1_scales)):
-            for q in quadrants:
-                nc.sync.dma_start(out=live_rows(w_plane[i], q), in_=scale_rows(scales, q))
+        for q in quadrants:
+            nc.sync.dma_start(out=live_rows(w_plane[1], q), in_=scale_rows(w2_scales, q))
+        nc.sync.dma_start(out=w_codes[0][:].bitcast(I32), in_=as_words(w1_words))
+        for q in quadrants:
+            nc.sync.dma_start(out=live_rows(w_plane[0], q), in_=scale_rows(w1_scales, q))
         nc.sync.dma_start(slot_t[:], slot)
 
         gain_bank = psum.tile([P, P], F32, name="gain_bank", tag=f"a{last}")
@@ -121,29 +122,22 @@ def tile_picked_momput_none_po_kernel(
 
         a_codes = sbuf("a_codes", [P, S], U32)
         a_plane = sbuf("a_plane", [P, S], U8)
-        a_codes_dealt = sbuf("a_codes_dealt", [P, S], U32)
-        a_plane_dealt = sbuf("a_plane_dealt", [P, S], U8)
         b_codes = [sbuf(f"b_codes{half}", [P, HALF], U32) for half in range(2)]
         b_plane = sbuf("b_plane", [P, V], U8)
 
-        def deal_tokens(dealt, picked):
-            nc.vector.tensor_copy(
-                out=dealt[:].rearrange("p (r c i) -> p c r i", r=PACK, i=LINE),
-                in_=picked[:].rearrange("p (c i r) -> p c r i", r=PACK, i=LINE),
-            )
+        def dealt(tokens):
+            return tokens[:].rearrange("p (r m) -> p m r", r=PACK)
 
+        nc.vector.tensor_copy(dealt(a_plane), x_plane[:].indirect(offs_t[:]))
         nc.vector.tensor_copy(b_plane[:], x_plane[:].indirect(two_t[:]))
-        nc.vector.tensor_copy(a_plane[:], x_plane[:].indirect(offs_t[:]))
-        deal_tokens(a_plane_dealt, a_plane)
         nc.vector.tensor_copy(b_codes[0][:], x_codes[:].indirect(entries(two_t, 0, HALF)))
-        nc.vector.tensor_copy(a_codes[:], x_codes[:].indirect(offs_t[:]))
-        deal_tokens(a_codes_dealt, a_codes)
+        nc.vector.tensor_copy(dealt(a_codes), x_codes[:].indirect(offs_t[:]))
         nc.vector.tensor_copy(b_codes[1][:], x_codes[:].indirect(entries(two_t, HALF, HALF)))
 
         page_rows = page.rearrange("(p r) c -> p r c", r=PACK)
         out_rows = out_0.rearrange("(p r) c -> p r c", r=PACK)
         window = {}
-        for r, freed in zip(ROW_TILES, ["w_codes1", "w_codes0", "a_codes", "x_codes"]):
+        for r, freed in zip(ROW_TILES, ["w_codes1", "w_codes0", "x_codes", "b_codes0"]):
             window[r] = sbuf(f"window{r}", [P, U], F32, after=freed)
             nc.sync.dma_start(out=window[r][:], in_=page_rows[:, r, :])
 
@@ -172,7 +166,7 @@ def tile_picked_momput_none_po_kernel(
 
         def project_a(r):
             for t in range(PACK):
-                project(a_bank[r][:, t, :], 0, t, a_codes_dealt[:, block(r, P)], a_plane_dealt[:, block(r, P)])
+                project(a_bank[r][:, t, :], 0, t, a_codes[:, block(r, P)], a_plane[:, block(r, P)])
 
         project_b(0)
         project_a(first)
@@ -184,7 +178,7 @@ def tile_picked_momput_none_po_kernel(
         z_grouped = {r: sbuf(f"z_grouped{r}", [P, P, PACK], BF16) for r in ROW_TILES}
         z_codes = sbuf("z_codes", [P, S], U32)
         z_plane = sbuf("z_plane", [P, S], U8)
-        z2_grouped = [sbuf(f"z2_grouped{half}", [P, HALF, PACK], BF16) for half in range(2)]
+        z2_grouped = [sbuf("z2_grouped0", [P, HALF, PACK], BF16)]
         z2_codes = sbuf("z2_codes", [P, V], U32)
         z2_plane = sbuf("z2_plane", [P, V], U8)
 
@@ -195,7 +189,9 @@ def tile_picked_momput_none_po_kernel(
             quantise(z_codes[:, block(r, P)], z_plane[:, block(r, P)], z_grouped[r][:])
 
         def quantise_z2(half):
-            quantise(z2_codes[:, block(half, HALF)], z2_plane[:, block(half, HALF)], z2_grouped[half][:])
+            for n in range(2):
+                cols = block(2 * half + n, P)
+                quantise(z2_codes[:, cols], z2_plane[:, cols], z2_grouped[half][:, block(n, P), :])
 
         def weigh(slots, t, sums, i):
             nc.scalar.activation(out=slots[:, t, :], in_=sums, func=ACT.Copy, scale=gains[:, i, t : t + 1])
@@ -228,6 +224,7 @@ def tile_picked_momput_none_po_kernel(
         weigh_and_group(z_grouped[first][:], a_bank[first], 0)
         quantise_z2(0)
         quantise_z(first)
+        z2_grouped.append(sbuf("z2_grouped1", [P, HALF, PACK], BF16, after=f"z_grouped{first}"))
         weigh_b(1)
         quantise_z2(1)
 

from contextlib import ExitStack

import concourse.mybir as mybir
from concourse.masks import make_identity

K, T, S, V, U, H = 512, 2048, 512, 512, 1024, 512
FLOPS = 2 * K * H * S + 2 * K * H * V + 2 * H * S * V

F32 = mybir.dt.float32
BF16 = mybir.dt.bfloat16
I32 = mybir.dt.int32
U32 = mybir.dt.uint32
U16 = mybir.dt.uint16
U8 = mybir.dt.uint8
FP8X4 = mybir.dt.float8_e4m3fn_x4
ACT = mybir.ActivationFunctionType

P = 128
PACK = 4
QUADRANT = 32
BLOCK_ROWS = 8
LIST_ROWS = 16
SCORE_SCALE = 0.0625
HALF = V // 2
LINE = 4

ROW_TILES = [0, 2, 3, 1]
VECTOR_COLUMNS = 768
PIECES = [slice(0, 512), slice(512, 768), slice(768, 1024)]


def as_words(packed):
    return packed[0].rearrange("p n r -> p (n r)").bitcast(I32)


def scale_rows(scales, quadrant):
    return scales[0, PACK * quadrant : PACK * (quadrant + 1), :].bitcast(I32)


def live_rows(plane, quadrant):
    return plane[QUADRANT * quadrant : QUADRANT * quadrant + PACK, :].bitcast(I32)


def entries(offsets, start, count):
    return offsets[:, start // LIST_ROWS : (start + count) // LIST_ROWS]


def block(index, width):
    return slice(index * width, (index + 1) * width)


def tile_picked_momput_none_po_kernel(
    tc, x_words, x_scales, w1_words, w1_scales, w2_words, w2_scales, ga, gb, page, offs, two, slot, out_0, out_1, out_2
):
    nc = tc.nc
    first, second, third, last = ROW_TILES
    quadrants = range(P // QUADRANT)
    with ExitStack() as ctx:
        lists = ctx.enter_context(tc.tile_pool(name="lists", bufs=1))
        keep = ctx.enter_context(tc.tile_pool(name="keep", bufs=1))
        psum = ctx.enter_context(tc.psum_pool(name="psum", bufs=1))

        def sbuf(name, shape, dtype, after=None):
            return keep.tile(shape, dtype, name=name, tag=after or name, align_bytes=64)

        offs_t = lists.tile([P, S // LIST_ROWS], U16, name="offs_t")
        two_t = lists.tile([P, V // LIST_ROWS], U16, name="two_t")
        slot_t = lists.tile([P, V // LIST_ROWS], U16, name="slot_t")

        identity = sbuf("identity", [P, P], F32)
        x_plane = sbuf("x_plane", [P, T], U8)
        x_codes = sbuf("x_codes", [P, T], U32)
        w_plane = [sbuf(f"w_plane{i}", [P, H], U8) for i in range(2)]
        w_codes = [sbuf(f"w_codes{i}", [P, H], U32) for i in range(2)]
        w_plane_dealt = [sbuf(f"w_plane_dealt{i}", [P, H], U8) for i in range(2)]
        w_codes_dealt = [sbuf(f"w_codes_dealt{i}", [P, H], U32) for i in range(2)]
        gain_rows = sbuf("gain_rows", [P, P], F32)
        gains = sbuf("gains", [P, 2, PACK], F32)

        nc.vector.memset(gain_rows[:], 0.0)
        for i in (1, 0):
            nc.vector.memset(w_plane[i][:].bitcast(I32), 0)
        sixteenth = sbuf("sixteenth", [P, 1], F32)
        nc.vector.memset(sixteenth[:], SCORE_SCALE)

        nc.sync.dma_start(offs_t[:], offs)
        for q in quadrants:
            nc.sync.dma_start(
                out=x_plane[block(q, QUADRANT), :].bitcast(I32),
                in_=scale_rows(x_scales, q).unsqueeze(0).to_broadcast([QUADRANT // PACK, PACK, T // PACK]),
            )
        nc.sync.dma_start(two_t[:], two)
        nc.sync.dma_start(out=x_codes[:].bitcast(I32), in_=as_words(x_words))
        make_identity(nc, identity[:])
        nc.sync.dma_start(out=w_codes[1][:].bitcast(I32), in_=as_words(w2_words))
        for i, gain in enumerate((ga, gb)):
            nc.sync.dma_start(
                out=gain_rows[block(i, PACK), :].rearrange("t (g j) -> t g j", j=BLOCK_ROWS),
                in_=gain.rearrange("(g t j) o -> t g (j o)", t=PACK, j=BLOCK_ROWS),
            )
        for q in quadrants:
            nc.sync.dma_start(out=live_rows(w_plane[1], q), in_=scale_rows(w2_scales, q))
        nc.sync.dma_start(out=w_codes[0][:].bitcast(I32), in_=as_words(w1_words))
        for q in quadrants:
            nc.sync.dma_start(out=live_rows(w_plane[0], q), in_=scale_rows(w1_scales, q))
        nc.sync.dma_start(slot_t[:], slot)

        gain_bank = psum.tile([P, P], F32, name="gain_bank", tag=f"a{last}")
        nc.tensor.transpose(gain_bank[:], gain_rows[:], identity[:])
        nc.scalar.copy(out=gains[:].rearrange("p i t -> p (i t)"), in_=gain_bank[:, 0 : 2 * PACK])

        for i in (1, 0):
            nc.scalar.copy(
                out=w_plane_dealt[i][:].bitcast(U32).rearrange("p (t g j) -> p t g j", t=PACK, j=BLOCK_ROWS // 4),
                in_=w_plane[i][:].bitcast(U32).rearrange("p (g t j) -> p t g j", t=PACK, j=BLOCK_ROWS // 4),
            )
            for slots in (slice(0, 2), slice(2, 4)):
                nc.scalar.copy(
                    out=w_codes_dealt[i][:].rearrange("p (t g j) -> p t g j", t=PACK, j=BLOCK_ROWS)[:, slots],
                    in_=w_codes[i][:].rearrange("p (g t j) -> p t g j", t=PACK, j=BLOCK_ROWS)[:, slots],
                )

        a_codes = sbuf("a_codes", [P, S], U32)
        a_plane = sbuf("a_plane", [P, S], U8)
        b_codes = [sbuf(f"b_codes{half}", [P, HALF], U32) for half in range(2)]
        b_plane = sbuf("b_plane", [P, V], U8)

        def dealt(tokens):
            return tokens[:].rearrange("p (r m) -> p m r", r=PACK)

        nc.vector.tensor_copy(dealt(a_plane), x_plane[:].indirect(offs_t[:]))
        nc.vector.tensor_copy(b_plane[:], x_plane[:].indirect(two_t[:]))
        nc.vector.tensor_copy(b_codes[0][:], x_codes[:].indirect(entries(two_t, 0, HALF)))
        nc.vector.tensor_copy(dealt(a_codes), x_codes[:].indirect(offs_t[:]))
        nc.vector.tensor_copy(b_codes[1][:], x_codes[:].indirect(entries(two_t, HALF, HALF)))

        page_rows = page.rearrange("(p r) c -> p r c", r=PACK)
        out_rows = out_0.rearrange("(p r) c -> p r c", r=PACK)
        window = {}
        for r, freed in zip(ROW_TILES, ["w_codes1", "w_codes0", "x_codes", "b_codes0"]):
            window[r] = sbuf(f"window{r}", [P, U], F32, after=freed)
            nc.sync.dma_start(out=window[r][:], in_=page_rows[:, r, :])

        def product(out, left_codes, left_plane, right_codes, right_plane):
            nc.tensor.matmul_mx(
                out=out,
                lhsT=left_codes.bitcast(FP8X4),
                lhsT_scale=left_plane,
                rhs=right_codes.bitcast(FP8X4),
                rhs_scale=right_plane,
                start=True,
                stop=True,
            )

        def project(out, i, t, codes, plane):
            product(out, w_codes_dealt[i][:, block(t, P)], w_plane_dealt[i][:, block(t, P)], codes, plane)

        b_bank = [psum.tile([P, PACK, P], F32, name=f"b_bank{n}", tag=f"b{n}") for n in range(V // P)]
        a_bank = {r: psum.tile([P, PACK, P], F32, name=f"a_bank{r}", tag=f"a{r}") for r in ROW_TILES}

        def project_b(half):
            for n in range(2):
                for t in range(PACK):
                    quarter = 2 * half + n
                    project(b_bank[quarter][:, t, :], 1, t, b_codes[half][:, block(n, P)], b_plane[:, block(quarter, P)])

        def project_a(r):
            for t in range(PACK):
                project(a_bank[r][:, t, :], 0, t, a_codes[:, block(r, P)], a_plane[:, block(r, P)])

        project_b(0)
        project_a(first)
        project_b(1)
        for r in ROW_TILES[1:]:
            project_a(r)

        z_slots = {r: sbuf(f"z_slots{r}", [P, PACK, P], BF16) for r in ROW_TILES[1:]}
        z_grouped = {r: sbuf(f"z_grouped{r}", [P, P, PACK], BF16) for r in ROW_TILES}
        z_codes = sbuf("z_codes", [P, S], U32)
        z_plane = sbuf("z_plane", [P, S], U8)
        z2_grouped = [sbuf("z2_grouped0", [P, HALF, PACK], BF16)]
        z2_codes = sbuf("z2_codes", [P, V], U32)
        z2_plane = sbuf("z2_plane", [P, V], U8)

        def quantise(codes, plane, grouped):
            nc.vector.quantize_mx(out=codes.bitcast(FP8X4), scales=plane, in_=grouped.rearrange("p c t -> p (c t)"))

        def quantise_z(r):
            quantise(z_codes[:, block(r, P)], z_plane[:, block(r, P)], z_grouped[r][:])

        def quantise_z2(half):
            for n in range(2):
                cols = block(2 * half + n, P)
                quantise(z2_codes[:, cols], z2_plane[:, cols], z2_grouped[half][:, block(n, P), :])

        def weigh(slots, t, sums, i):
            nc.scalar.activation(out=slots[:, t, :], in_=sums, func=ACT.Copy, scale=gains[:, i, t : t + 1])

        def group(copy, grouped, slots):
            copy(
                out=grouped[:].rearrange("p (c i) t -> p c t i", i=LINE),
                in_=slots[:].rearrange("p t (c i) -> p c t i", i=LINE),
            )

        def weigh_and_group(grouped, bank, i):
            nc.vector.tensor_tensor(
                out=grouped,
                in0=bank[:].rearrange("p t c -> p c t"),
                in1=gains[:, i, :].unsqueeze(1).to_broadcast([P, P, PACK]),
                op=mybir.AluOpType.mult,
            )

        def weigh_b(half):
            for n in range(2):
                weigh_and_group(z2_grouped[half][:, block(n, P), :], b_bank[2 * half + n], 1)

        def prepare_z(r):
            for t in range(PACK):
                weigh(z_slots[r], t, a_bank[r][:, t, :], 0)
            group(nc.scalar.copy, z_grouped[r], z_slots[r])
            quantise_z(r)

        weigh_b(0)
        weigh_and_group(z_grouped[first][:], a_bank[first], 0)
        quantise_z2(0)
        quantise_z(first)
        z2_grouped.append(sbuf("z2_grouped1", [P, HALF, PACK], BF16, after=f"z_grouped{first}"))
        weigh_b(1)
        quantise_z2(1)

        y_codes = sbuf("y_codes", [P, U], U32)
        y_plane = sbuf("y_plane", [P, U], U8)

        def score(r, start, count, bank, scale, after=None):
            cols = slice(start, start + count)
            cv = psum.tile([P, count], F32, name=f"cv{r}_{start}", tag=bank)
            product(cv[:], z_codes[:, block(r, P)], z_plane[:, block(r, P)], z2_codes[:, cols], z2_plane[:, cols])
            values = sbuf(f"tanh{r}_{start}", [P, count], F32, after=after)
            nc.scalar.activation(out=values[:], in_=cv[:], func=ACT.Tanh, scale=scale)
            return values

        def put(r, start, count, values):
            nc.vector.tensor_copy(window[r][:].indirect(entries(slot_t, start, count)), values[:])

        first_half = score(first, 0, HALF, "b0", sixteenth[:])
        prepare_z(second)
        prepare_z(third)
        second_half = score(first, HALF, HALF, "b1", sixteenth[:], after=f"z_slots{third}")
        prepare_z(last)
        values = {second: score(second, 0, V, "b2", sixteenth[:], after=f"z_slots{last}")}
        values[third] = score(third, 0, V, "b3", sixteenth[:], after=f"z_grouped{last}")

        y_grouped = sbuf("y_grouped", [P, U, PACK], BF16, after="sixteenth")

        def regroup(copy, r, cols):
            copy(out=y_grouped[:, cols, r], in_=window[r][:, cols])

        put(first, 0, HALF, first_half)
        put(first, HALF, HALF, second_half)
        nc.sync.dma_start(out=out_rows[:, first, :], in_=window[first][:])
        for done, r in zip(ROW_TILES, ROW_TILES[1:]):
            for cols in ([slice(0, U)] if done == first else [block(half, U // 2) for half in range(2)]):
                regroup(nc.scalar.copy, done, cols)
            if done == first:
                values[last] = score(last, 0, V, "b3", SCORE_SCALE)
            put(r, 0, V, values[r])
            nc.sync.dma_start(out=out_rows[:, r, :], in_=window[r][:])

        for cols in PIECES:
            regroup(nc.vector.tensor_copy if cols.stop <= VECTOR_COLUMNS else nc.scalar.copy, last, cols)
        for cols in PIECES:
            quantise(y_codes[:, cols], y_plane[:, cols], y_grouped[:, cols, :])
            nc.sync.dma_start(out=as_words(out_1)[:, cols], in_=y_codes[:, cols].bitcast(I32))
        for q in quadrants:
            queue = nc.scalar if q % 2 else nc.sync
            queue.dma_start(out=scale_rows(out_2, q), in_=live_rows(y_plane, q))
